import numpy as np
import ml_dtypes


def mxq(x, axis, fmt="e4m3"):
    dtype, down = {"e4m3": (ml_dtypes.float8_e4m3fn, 7), "e5m2": (ml_dtypes.float8_e5m2, 14)}[fmt]
    v = np.moveaxis(np.asarray(x, np.float32).astype(ml_dtypes.bfloat16).astype(np.float64), axis, -1)
    blocks = v.reshape(v.shape[:-1] + (-1, 32))
    amax = np.abs(blocks).max(-1, keepdims=True)
    byte = np.maximum(np.where(amax > 0, np.frexp(amax)[1] - 1 + 127, 0) - down, 1)
    scale = np.exp2(byte - 127.0)
    codes = (blocks / scale).astype(np.float32).astype(dtype).astype(np.float64)
    return np.moveaxis((codes * scale).reshape(v.shape), -1, axis)


WIDE = False


def mx_kscale(k):
    if not WIDE:
        return np.ones(k)
    levels = np.array([10, -10, 5, -5, 0])
    if k % 512:
        return np.exp2(np.random.permutation(np.resize(levels, k // 32))).repeat(32)
    a = np.empty((k // 512, 16))
    for p in range(k // 512):
        a[p, :8] = np.random.permutation(np.resize(levels, 8))
        for g in range(8):
            far = levels[np.abs(levels - a[p, g]) >= 10]
            a[p, g + 8] = far[np.random.randint(len(far))]
    return np.exp2(a.ravel()).repeat(32)


def f64(x):
    return np.asarray(x).astype(np.float64)


def striped(idx):
    return np.tile(idx.reshape(-1, 16).T, (8, 1)).astype(np.uint16)


def unstriped(offs):
    return offs[:16].T.reshape(-1).astype(np.int64)


def pack_weight(w):
    k, n = w.shape
    w = f64(np.asarray(w, np.float32).astype(ml_dtypes.bfloat16)).reshape(k // 32, 32, n)
    amax = np.abs(w).max(1)
    byte = np.clip(np.where(amax > 0, np.frexp(amax)[1] - 1 + 127 - 7, 1), 1, 254)
    scaled = (w * np.exp2(127.0 - byte)[:, None, :]).reshape(k, n).astype(np.float32)
    words = np.ascontiguousarray(scaled.reshape(k // 512, 128, 4, n).transpose(0, 1, 3, 2)).astype(ml_dtypes.float8_e4m3fn).view(np.uint8)
    return words, np.ascontiguousarray(byte.astype(np.uint8).reshape(k // 512, 16, n))


def unpack_weight(words, scales):
    g, p, n, _ = words.shape
    vals = np.ascontiguousarray(words).view(ml_dtypes.float8_e4m3fn).astype(np.float64) * np.repeat(np.exp2(scales.astype(np.float64) - 127.0), 8, axis=1)[..., None]
    return vals.transpose(0, 1, 3, 2).reshape(g * 512, n)


def relu(v):
    return np.maximum(v, 0.0)


K, T, S, V, R = 1024, 1024, 512, 256, 256


def setup_inputs():
    n = np.random.standard_normal
    s = mx_kscale(K)[:, None]
    c = mx_kscale(S)
    packed_xT = pack_weight(n((K, T)) * s)
    return {
        "x_words": packed_xT[0],
        "x_scales": packed_xT[1],
        "qT": (n((K, V)) / np.sqrt(K) / s).astype(np.float32),
        "term": (np.random.uniform(0.0, 2.0, (S, R)) / S / c[:, None]).astype(np.float32),
        "prior": (0.4 * n((S, 1))).astype(np.float32),
        "lenw": (np.random.uniform(0.5, 1.5, (S, 1)) * c[:, None]).astype(np.float32),
        "orig": (np.random.uniform(0.0, 2.0, (R, V))).astype(np.float32),
        "idf": (np.random.uniform(0.4, 2.0, (R, 1))).astype(np.float32),
        "offs": striped(np.random.permutation(T)[:S]),
    }


def reference(x_words, x_scales, qT, term, prior, lenw, orig, idf, offs):
    xq = unpack_weight(x_words, x_scales)[:, unstriped(offs)]
    qTq = mxq(f64(qT), 0, "e4m3")
    y = xq.T @ qTq
    pd = relu(y + f64(prior))
    wd = f64(lenw) * pd
    fb = mxq(f64(term), 0, "e4m3").T @ mxq(wd, 0, "e4m3")
    return (fb / (fb + 0.6)) * (f64(idf) * f64(orig))

@@ -1,0 +1,185 @@
+from contextlib import ExitStack
+
+import concourse.mybir as mybir
+
+K, T, S, V, R = 1024, 1024, 512, 256, 256
+SATURATION = 0.6
+FLOPS = 2 * K * S * V + 2 * S * R * V
+
+F32 = mybir.dt.float32
+BF16 = mybir.dt.bfloat16
+I32 = mybir.dt.int32
+U32 = mybir.dt.uint32
+U16 = mybir.dt.uint16
+U8 = mybir.dt.uint8
+FP8X4 = mybir.dt.float8_e4m3fn_x4
+ACT = mybir.ActivationFunctionType
+ALU = mybir.AluOpType
+
+P = 128
+PACK = 4
+PASSES = K // (P * PACK)
+HALVES = 2
+VH = V // HALVES
+R_BLOCKS = R // P
+
+
+def interleave_views(dst, src):
+    return (
+        dst.rearrange("p (c i) j -> p c j i", i=4),
+        src.rearrange("p j (c i) -> p c j i", i=4),
+    )
+
+
+def tile_picked_yrm3_sat_p_kernel(
+    tc, x_words, x_scales, qT, term, prior, lenw, orig, idf, offs, out
+):
+    nc = tc.nc
+    with ExitStack() as ctx:
+        keep = ctx.enter_context(tc.tile_pool(name="keep", bufs=1))
+        psum = ctx.enter_context(tc.psum_pool(name="psum", bufs=1))
+
+        def sb(name, shape, dtype):
+            return keep.tile(shape, dtype, name=name, align_bytes=64)
+
+        scale_table = sb("scale_table", [P, T], U8)
+        nc.vector.memset(scale_table[:].bitcast(I32), 0)
+        warm_in = sb("warm_in", [P, 1], F32)
+        warm_out = sb("warm_out", [P, 1], F32)
+        nc.gpsimd.memset(warm_in[:], 1.0)
+        nc.scalar.activation(out=warm_out[:], in_=warm_in[:], func=ACT.Abs_reciprocal_sqrt)
+
+        offsets = keep.tile([P, S // 16], U16, name="offsets")
+        nc.sync.dma_start(offsets[:], offs)
+        prior_sb = sb("prior_sb", [P, PACK], F32)
+        lenw_sb = sb("lenw_sb", [P, PACK], F32)
+        idf_sb = sb("idf_sb", [P, R_BLOCKS], F32)
+        for quad in range(4):
+            nc.sync.dma_start(
+                out=scale_table[32 * quad : 32 * quad + 4 * PASSES, :].bitcast(I32),
+                in_=x_scales[:, 4 * quad : 4 * quad + 4, :].bitcast(I32),
+            )
+
+        word_table = [sb(f"word_table{o}", [P, T], I32) for o in range(PASSES)]
+        q_rows = qT.rearrange("(o p j) v -> o p j v", p=P, j=PACK)
+        q0_raw = sb("q0_raw", [P, PACK, V], F32)
+        q1_raw = [sb(f"q1_raw{h}", [P, PACK, VH], F32) for h in range(HALVES)]
+        q_raw = [[q0_raw[:, :, h * VH : (h + 1) * VH] for h in range(HALVES)], [q1_raw[h][:] for h in range(HALVES)]]
+        term_raw = sb("term_raw", [P, PACK, R], F32)
+        orig_sb = sb("orig_sb", [P, R_BLOCKS, V], F32)
+
+        def load_words(o):
+            nc.sync.dma_start(out=word_table[o][:], in_=x_words[o].rearrange("p c j -> p (c j)").bitcast(I32))
+
+        load_words(0)
+        nc.sync.dma_start(out=q0_raw[:], in_=q_rows[0])
+        load_words(1)
+        nc.sync.dma_start(out=prior_sb[:], in_=prior.rearrange("(p j) one -> p (j one)", j=PACK))
+        nc.sync.dma_start(out=lenw_sb[:], in_=lenw.rearrange("(p j) one -> p (j one)", j=PACK))
+        for h in range(HALVES):
+            nc.sync.dma_start(out=q1_raw[h][:], in_=q_rows[1][:, :, h * VH : (h + 1) * VH])
+        nc.sync.dma_start(out=term_raw[:], in_=term.rearrange("(p j) r -> p j r", j=PACK))
+        nc.sync.dma_start(out=orig_sb[:], in_=orig.rearrange("(b p) v -> p b v", p=P))
+        with nc.allow_non_contiguous_dma(reason="one value a partition and row block"):
+            nc.sync.dma_start(out=idf_sb[:], in_=idf.rearrange("(b p) one -> p (b one)", p=P))
+        bias_sb = sb("bias_sb", [P, PACK], F32)
+        nc.gpsimd.tensor_tensor(out=bias_sb[:], in0=prior_sb[:], in1=lenw_sb[:], op=ALU.mult)
+
+        picked_scales = sb("picked_scales", [P, S], U8)
+        x_scale = sb("x_scale", [P, S], U8)
+        nc.vector.tensor_copy(out=picked_scales[:], in_=scale_table[:].indirect(offsets[:]))
+        nc.vector.tensor_copy(
+            out=x_scale[:].rearrange("p (j m) -> p j m", j=PACK),
+            in_=picked_scales[:].rearrange("p (m j) -> p j m", j=PACK),
+        )
+        x_codes = [sb(f"x_codes{o}", [P, S], U32) for o in range(PASSES)]
+
+        def gather_words(o):
+            nc.vector.tensor_copy(
+                out=x_codes[o][:].rearrange("p (j m) -> p m j", j=PACK),
+                in_=word_table[o][:].bitcast(U32).indirect(offsets[:]),
+            )
+
+        def quantize(name, grouped, width):
+            codes = sb(name + "_codes", [P, width], U32)
+            scales = sb(name + "_scales", [P, width], U8)
+            nc.vector.quantize_mx(
+                out=codes[:].bitcast(FP8X4), scales=scales[:], in_=grouped[:].rearrange("p c j -> p (c j)")
+            )
+            return codes, scales
+
+        y_bank = [[psum.tile([P, VH], F32, name=f"y{h}{j}", tag=f"bank{h}{j}") for j in range(PACK)] for h in range(HALVES)]
+
+        def first_product(o, h, codes, scales):
+            for j in range(PACK):
+                cols = slice(j * P, (j + 1) * P)
+                nc.tensor.matmul_mx(
+                    out=y_bank[h][j][:],
+                    lhsT=x_codes[o][:, cols].bitcast(FP8X4),
+                    lhsT_scale=x_scale[4 * o :, cols],
+                    rhs=codes.bitcast(FP8X4),
+                    rhs_scale=scales,
+                    start=(o == 0),
+                    stop=(o == PASSES - 1),
+                )
+
+        for o in range(PASSES):
+            gather_words(o)
+            for h in range(HALVES):
+                q_bf = sb(f"q_bf{o}{h}", [P, VH, PACK], BF16)
+                dst, src = interleave_views(q_bf[:], q_raw[o][h])
+                if (o, h) == (1, 1):
+                    nc.vector.tensor_copy(out=dst, in_=src)
+                else:
+                    nc.scalar.copy(out=dst, in_=src)
+                codes, scales = quantize(f"q{o}{h}", q_bf, VH)
+                first_product(o, h, codes[:], scales[:])
+
+        wd_rows = [sb(f"wd_rows{h}", [P, PACK, VH], BF16) for h in range(HALVES)]
+        wd_bf = [sb(f"wd_bf{h}", [P, VH, PACK], BF16) for h in range(HALVES)]
+        for h in range(HALVES):
+            for j in range(PACK):
+                nc.scalar.activation(
+                    out=wd_rows[h][:, j, :], in_=y_bank[h][j][:], func=ACT.Relu,
+                    scale=lenw_sb[:, j : j + 1], bias=bias_sb[:, j : j + 1],
+                )
+
+        term_bf = sb("term_bf", [P, R, PACK], BF16)
+        dst, src = interleave_views(term_bf[:], term_raw[:])
+        nc.vector.tensor_copy(out=dst, in_=src)
+        dst, src = interleave_views(wd_bf[0][:], wd_rows[0][:])
+        nc.vector.tensor_copy(out=dst, in_=src)
+        term_codes, term_scales = quantize("term", term_bf, R)
+        dst, src = interleave_views(wd_bf[1][:], wd_rows[1][:])
+        nc.scalar.copy(out=dst, in_=src)
+        wd_q = [quantize(f"wd{h}", wd_bf[h], VH) for h in range(HALVES)]
+
+        out_rows = out.rearrange("(b p) v -> p b v", p=P)
+        for h in range(HALVES):
+            cols = slice(h * VH, (h + 1) * VH)
+            fb = []
+            for b in range(R_BLOCKS):
+                fb.append(psum.tile([P, VH], F32, name=f"fb{h}{b}", tag=f"bank{h}{b}"))
+                nc.tensor.matmul_mx(
+                    out=fb[b][:],
+                    lhsT=term_codes[:, b * P : (b + 1) * P].bitcast(FP8X4),
+                    lhsT_scale=term_scales[:, b * P : (b + 1) * P],
+                    rhs=wd_q[h][0][:].bitcast(FP8X4),
+                    rhs_scale=wd_q[h][1][:],
+                    start=True,
+                    stop=True,
+                )
+            root = sb(f"root{h}", [P, R_BLOCKS, VH], F32)
+            numer = sb(f"numer{h}", [P, R_BLOCKS, VH], F32)
+            inverse = sb(f"inverse{h}", [P, R_BLOCKS, VH], F32)
+            result = sb(f"result{h}", [P, R_BLOCKS, VH], F32)
+            for b in range(R_BLOCKS):
+                nc.scalar.activation(out=root[:, b, :], in_=fb[b][:], func=ACT.Abs_reciprocal_sqrt, bias=SATURATION)
+            for b in range(R_BLOCKS):
+                nc.vector.scalar_tensor_tensor(
+                    out=numer[:, b, :], in0=fb[b][:], scalar=idf_sb[:, b : b + 1],
+                    in1=orig_sb[:, b, cols], op0=ALU.mult, op1=ALU.mult,
+                )
+            nc.scalar.activation(out=inverse[:], in_=root[:], func=ACT.Square)
+            nc.vector.tensor_tensor(out=result[:], in0=numer[:], in1=inverse[:], op=ALU.mult)
+            nc.sync.dma_start(out=out_rows[:, :, cols], in_=result[:])

@@ -22,6 +22,7 @@ PASSES = K // (P * PACK)
 HALVES = 2
 VH = V // HALVES
 R_BLOCKS = R // P
+SCALAR_COLS = 48
 
 
 def interleave_views(dst, src):
@@ -40,13 +41,13 @@ def tile_picked_yrm3_sat_p_kernel(
         psum = ctx.enter_context(tc.psum_pool(name="psum", bufs=1))
 
         def sb(name, shape, dtype):
-            return keep.tile(shape, dtype, name=name, align_bytes=64)
+            return keep.tile(shape, dtype, name=name, tag=name, align_bytes=64)
 
         scale_table = sb("scale_table", [P, T], U8)
         nc.vector.memset(scale_table[:].bitcast(I32), 0)
         warm_in = sb("warm_in", [P, 1], F32)
         warm_out = sb("warm_out", [P, 1], F32)
-        nc.gpsimd.memset(warm_in[:], 1.0)
+        nc.vector.memset(warm_in[:], 1.0)
         nc.scalar.activation(out=warm_out[:], in_=warm_in[:], func=ACT.Abs_reciprocal_sqrt)
 
         offsets = keep.tile([P, S // 16], U16, name="offsets")
@@ -62,36 +63,28 @@ def tile_picked_yrm3_sat_p_kernel(
 
         word_table = [sb(f"word_table{o}", [P, T], I32) for o in range(PASSES)]
         q_rows = qT.rearrange("(o p j) v -> o p j v", p=P, j=PACK)
-        q0_raw = sb("q0_raw", [P, PACK, V], F32)
-        q1_raw = [sb(f"q1_raw{h}", [P, PACK, VH], F32) for h in range(HALVES)]
-        q_raw = [[q0_raw[:, :, h * VH : (h + 1) * VH] for h in range(HALVES)], [q1_raw[h][:] for h in range(HALVES)]]
+        q_raw = [sb(f"q_raw{o}", [P, PACK, V], F32) for o in range(PASSES)]
         term_raw = sb("term_raw", [P, PACK, R], F32)
         orig_sb = sb("orig_sb", [P, R_BLOCKS, V], F32)
 
-        def load_words(o):
+        for o in range(PASSES):
             nc.sync.dma_start(out=word_table[o][:], in_=x_words[o].rearrange("p c j -> p (c j)").bitcast(I32))
-
-        load_words(0)
-        nc.sync.dma_start(out=q0_raw[:], in_=q_rows[0])
-        load_words(1)
-        nc.sync.dma_start(out=prior_sb[:], in_=prior.rearrange("(p j) one -> p (j one)", j=PACK))
-        nc.sync.dma_start(out=lenw_sb[:], in_=lenw.rearrange("(p j) one -> p (j one)", j=PACK))
-        for h in range(HALVES):
-            nc.sync.dma_start(out=q1_raw[h][:], in_=q_rows[1][:, :, h * VH : (h + 1) * VH])
+            if o == PASSES - 1:
+                nc.sync.dma_start(out=prior_sb[:], in_=prior.rearrange("(p j) one -> p (j one)", j=PACK))
+                nc.sync.dma_start(out=lenw_sb[:], in_=lenw.rearrange("(p j) one -> p (j one)", j=PACK))
+            nc.sync.dma_start(out=q_raw[o][:], in_=q_rows[o])
         nc.sync.dma_start(out=term_raw[:], in_=term.rearrange("(p j) r -> p j r", j=PACK))
         nc.sync.dma_start(out=orig_sb[:], in_=orig.rearrange("(b p) v -> p b v", p=P))
         with nc.allow_non_contiguous_dma(reason="one value a partition and row block"):
             nc.sync.dma_start(out=idf_sb[:], in_=idf.rearrange("(b p) one -> p (b one)", p=P))
         bias_sb = sb("bias_sb", [P, PACK], F32)
-        nc.gpsimd.tensor_tensor(out=bias_sb[:], in0=prior_sb[:], in1=lenw_sb[:], op=ALU.mult)
+        for j in range(PACK):
+            nc.scalar.activation(
+                out=bias_sb[:, j : j + 1], in_=prior_sb[:, j : j + 1], func=ACT.Copy, scale=lenw_sb[:, j : j + 1]
+            )
 
         picked_scales = sb("picked_scales", [P, S], U8)
-        x_scale = sb("x_scale", [P, S], U8)
         nc.vector.tensor_copy(out=picked_scales[:], in_=scale_table[:].indirect(offsets[:]))
-        nc.vector.tensor_copy(
-            out=x_scale[:].rearrange("p (j m) -> p j m", j=PACK),
-            in_=picked_scales[:].rearrange("p (m j) -> p j m", j=PACK),
-        )
         x_codes = [sb(f"x_codes{o}", [P, S], U32) for o in range(PASSES)]
 
         def gather_words(o):
@@ -123,12 +116,19 @@ def tile_picked_yrm3_sat_p_kernel(
                     stop=(o == PASSES - 1),
                 )
 
+        gather_words(0)
+        x_scale = keep.tile([P, S], U8, name="x_scale", tag="word_table0", align_bytes=64)
+        nc.vector.tensor_copy(
+            out=x_scale[:].rearrange("p (j m) -> p j m", j=PACK),
+            in_=picked_scales[:].rearrange("p (m j) -> p j m", j=PACK),
+        )
         for o in range(PASSES):
-            gather_words(o)
+            if o > 0:
+                gather_words(o)
             for h in range(HALVES):
                 q_bf = sb(f"q_bf{o}{h}", [P, VH, PACK], BF16)
-                dst, src = interleave_views(q_bf[:], q_raw[o][h])
-                if (o, h) == (1, 1):
+                dst, src = interleave_views(q_bf[:], q_raw[o][:, :, h * VH : (h + 1) * VH])
+                if (o, h) == (PASSES - 1, HALVES - 1):
                     nc.vector.tensor_copy(out=dst, in_=src)
                 else:
                     nc.scalar.copy(out=dst, in_=src)
@@ -150,18 +150,20 @@ def tile_picked_yrm3_sat_p_kernel(
         dst, src = interleave_views(wd_bf[0][:], wd_rows[0][:])
         nc.vector.tensor_copy(out=dst, in_=src)
         term_codes, term_scales = quantize("term", term_bf, R)
-        dst, src = interleave_views(wd_bf[1][:], wd_rows[1][:])
+        wd_q = [quantize("wd0", wd_bf[0], VH)]
+        dst, src = interleave_views(wd_bf[1][:, :SCALAR_COLS, :], wd_rows[1][:, :, :SCALAR_COLS])
         nc.scalar.copy(out=dst, in_=src)
-        wd_q = [quantize(f"wd{h}", wd_bf[h], VH) for h in range(HALVES)]
+        dst, src = interleave_views(wd_bf[1][:, SCALAR_COLS:, :], wd_rows[1][:, :, SCALAR_COLS:])
+        nc.vector.tensor_copy(out=dst, in_=src)
+        wd_q.append(quantize("wd1", wd_bf[1], VH))
 
         out_rows = out.rearrange("(b p) v -> p b v", p=P)
         for h in range(HALVES):
             cols = slice(h * VH, (h + 1) * VH)
-            fb = []
+            fb = psum.tile([P, R_BLOCKS, VH], F32, name=f"fb{h}", tag=f"bank{h}0")
             for b in range(R_BLOCKS):
-                fb.append(psum.tile([P, VH], F32, name=f"fb{h}{b}", tag=f"bank{h}{b}"))
                 nc.tensor.matmul_mx(
-                    out=fb[b][:],
+                    out=fb[:, b, :],
                     lhsT=term_codes[:, b * P : (b + 1) * P].bitcast(FP8X4),
                     lhsT_scale=term_scales[:, b * P : (b + 1) * P],
                     rhs=wd_q[h][0][:].bitcast(FP8X4),
@@ -173,11 +175,10 @@ def tile_picked_yrm3_sat_p_kernel(
             numer = sb(f"numer{h}", [P, R_BLOCKS, VH], F32)
             inverse = sb(f"inverse{h}", [P, R_BLOCKS, VH], F32)
             result = sb(f"result{h}", [P, R_BLOCKS, VH], F32)
-            for b in range(R_BLOCKS):
-                nc.scalar.activation(out=root[:, b, :], in_=fb[b][:], func=ACT.Abs_reciprocal_sqrt, bias=SATURATION)
+            nc.scalar.activation(out=root[:], in_=fb[:], func=ACT.Abs_reciprocal_sqrt, bias=SATURATION)
             for b in range(R_BLOCKS):
                 nc.vector.scalar_tensor_tensor(
-                    out=numer[:, b, :], in0=fb[b][:], scalar=idf_sb[:, b : b + 1],
+                    out=numer[:, b, :], in0=fb[:, b, :], scalar=idf_sb[:, b : b + 1],
                     in1=orig_sb[:, b, cols], op0=ALU.mult, op1=ALU.mult,
                 )
             nc.scalar.activation(out=inverse[:], in_=root[:], func=ACT.Square)

from contextlib import ExitStack

import concourse.mybir as mybir

K, T, S, V, R = 1024, 1024, 512, 256, 256
SATURATION = 0.6
FLOPS = 2 * K * S * V + 2 * S * R * V

F32 = mybir.dt.float32
BF16 = mybir.dt.bfloat16
I32 = mybir.dt.int32
U32 = mybir.dt.uint32
U16 = mybir.dt.uint16
U8 = mybir.dt.uint8
FP8X4 = mybir.dt.float8_e4m3fn_x4
ACT = mybir.ActivationFunctionType
ALU = mybir.AluOpType

P = 128
PACK = 4
PASSES = K // (P * PACK)
HALVES = 2
VH = V // HALVES
R_BLOCKS = R // P
SCALAR_COLS = 48


def interleave_views(dst, src):
    return (
        dst.rearrange("p (c i) j -> p c j i", i=4),
        src.rearrange("p j (c i) -> p c j i", i=4),
    )


def tile_picked_yrm3_sat_p_kernel(
    tc, x_words, x_scales, qT, term, prior, lenw, orig, idf, offs, out
):
    nc = tc.nc
    with ExitStack() as ctx:
        keep = ctx.enter_context(tc.tile_pool(name="keep", bufs=1))
        psum = ctx.enter_context(tc.psum_pool(name="psum", bufs=1))

        def sb(name, shape, dtype):
            return keep.tile(shape, dtype, name=name, tag=name, align_bytes=64)

        scale_table = sb("scale_table", [P, T], U8)
        nc.vector.memset(scale_table[:].bitcast(I32), 0)
        warm_in = sb("warm_in", [P, 1], F32)
        warm_out = sb("warm_out", [P, 1], F32)
        nc.vector.memset(warm_in[:], 1.0)
        nc.scalar.activation(out=warm_out[:], in_=warm_in[:], func=ACT.Abs_reciprocal_sqrt)

        offsets = keep.tile([P, S // 16], U16, name="offsets")
        nc.sync.dma_start(offsets[:], offs)
        prior_sb = sb("prior_sb", [P, PACK], F32)
        lenw_sb = sb("lenw_sb", [P, PACK], F32)
        idf_sb = sb("idf_sb", [P, R_BLOCKS], F32)
        for quad in range(4):
            nc.sync.dma_start(
                out=scale_table[32 * quad : 32 * quad + 4 * PASSES, :].bitcast(I32),
                in_=x_scales[:, 4 * quad : 4 * quad + 4, :].bitcast(I32),
            )

        word_table = [sb(f"word_table{o}", [P, T], I32) for o in range(PASSES)]
        q_rows = qT.rearrange("(o p j) v -> o p j v", p=P, j=PACK)
        q_raw = [sb(f"q_raw{o}", [P, PACK, V], F32) for o in range(PASSES)]
        term_raw = sb("term_raw", [P, PACK, R], F32)
        orig_sb = sb("orig_sb", [P, R_BLOCKS, V], F32)

        for o in range(PASSES):
            nc.sync.dma_start(out=word_table[o][:], in_=x_words[o].rearrange("p c j -> p (c j)").bitcast(I32))
            if o == PASSES - 1:
                nc.sync.dma_start(out=prior_sb[:], in_=prior.rearrange("(p j) one -> p (j one)", j=PACK))
                nc.sync.dma_start(out=lenw_sb[:], in_=lenw.rearrange("(p j) one -> p (j one)", j=PACK))
            nc.sync.dma_start(out=q_raw[o][:], in_=q_rows[o])
        nc.sync.dma_start(out=term_raw[:], in_=term.rearrange("(p j) r -> p j r", j=PACK))
        nc.sync.dma_start(out=orig_sb[:], in_=orig.rearrange("(b p) v -> p b v", p=P))
        with nc.allow_non_contiguous_dma(reason="one value a partition and row block"):
            nc.sync.dma_start(out=idf_sb[:], in_=idf.rearrange("(b p) one -> p (b one)", p=P))
        bias_sb = sb("bias_sb", [P, PACK], F32)
        for j in range(PACK):
            nc.scalar.activation(
                out=bias_sb[:, j : j + 1], in_=prior_sb[:, j : j + 1], func=ACT.Copy, scale=lenw_sb[:, j : j + 1]
            )

        picked_scales = sb("picked_scales", [P, S], U8)
        nc.vector.tensor_copy(out=picked_scales[:], in_=scale_table[:].indirect(offsets[:]))
        x_codes = [sb(f"x_codes{o}", [P, S], U32) for o in range(PASSES)]

        def gather_words(o):
            nc.vector.tensor_copy(
                out=x_codes[o][:].rearrange("p (j m) -> p m j", j=PACK),
                in_=word_table[o][:].bitcast(U32).indirect(offsets[:]),
            )

        def quantize(name, grouped, width):
            codes = sb(name + "_codes", [P, width], U32)
            scales = sb(name + "_scales", [P, width], U8)
            nc.vector.quantize_mx(
                out=codes[:].bitcast(FP8X4), scales=scales[:], in_=grouped[:].rearrange("p c j -> p (c j)")
            )
            return codes, scales

        y_bank = [[psum.tile([P, VH], F32, name=f"y{h}{j}", tag=f"bank{h}{j}") for j in range(PACK)] for h in range(HALVES)]

        def first_product(o, h, codes, scales):
            for j in range(PACK):
                cols = slice(j * P, (j + 1) * P)
                nc.tensor.matmul_mx(
                    out=y_bank[h][j][:],
                    lhsT=x_codes[o][:, cols].bitcast(FP8X4),
                    lhsT_scale=x_scale[4 * o :, cols],
                    rhs=codes.bitcast(FP8X4),
                    rhs_scale=scales,
                    start=(o == 0),
                    stop=(o == PASSES - 1),
                )

        gather_words(0)
        x_scale = keep.tile([P, S], U8, name="x_scale", tag="word_table0", align_bytes=64)
        nc.vector.tensor_copy(
            out=x_scale[:].rearrange("p (j m) -> p j m", j=PACK),
            in_=picked_scales[:].rearrange("p (m j) -> p j m", j=PACK),
        )
        for o in range(PASSES):
            if o > 0:
                gather_words(o)
            for h in range(HALVES):
                q_bf = sb(f"q_bf{o}{h}", [P, VH, PACK], BF16)
                dst, src = interleave_views(q_bf[:], q_raw[o][:, :, h * VH : (h + 1) * VH])
                if (o, h) == (PASSES - 1, HALVES - 1):
                    nc.vector.tensor_copy(out=dst, in_=src)
                else:
                    nc.scalar.copy(out=dst, in_=src)
                codes, scales = quantize(f"q{o}{h}", q_bf, VH)
                first_product(o, h, codes[:], scales[:])

        wd_rows = [sb(f"wd_rows{h}", [P, PACK, VH], BF16) for h in range(HALVES)]
        wd_bf = [sb(f"wd_bf{h}", [P, VH, PACK], BF16) for h in range(HALVES)]
        for h in range(HALVES):
            for j in range(PACK):
                nc.scalar.activation(
                    out=wd_rows[h][:, j, :], in_=y_bank[h][j][:], func=ACT.Relu,
                    scale=lenw_sb[:, j : j + 1], bias=bias_sb[:, j : j + 1],
                )

        term_bf = sb("term_bf", [P, R, PACK], BF16)
        dst, src = interleave_views(term_bf[:], term_raw[:])
        nc.vector.tensor_copy(out=dst, in_=src)
        dst, src = interleave_views(wd_bf[0][:], wd_rows[0][:])
        nc.vector.tensor_copy(out=dst, in_=src)
        term_codes, term_scales = quantize("term", term_bf, R)
        wd_q = [quantize("wd0", wd_bf[0], VH)]
        dst, src = interleave_views(wd_bf[1][:, :SCALAR_COLS, :], wd_rows[1][:, :, :SCALAR_COLS])
        nc.scalar.copy(out=dst, in_=src)
        dst, src = interleave_views(wd_bf[1][:, SCALAR_COLS:, :], wd_rows[1][:, :, SCALAR_COLS:])
        nc.vector.tensor_copy(out=dst, in_=src)
        wd_q.append(quantize("wd1", wd_bf[1], VH))

        out_rows = out.rearrange("(b p) v -> p b v", p=P)
        for h in range(HALVES):
            cols = slice(h * VH, (h + 1) * VH)
            fb = psum.tile([P, R_BLOCKS, VH], F32, name=f"fb{h}", tag=f"bank{h}0")
            for b in range(R_BLOCKS):
                nc.tensor.matmul_mx(
                    out=fb[:, b, :],
                    lhsT=term_codes[:, b * P : (b + 1) * P].bitcast(FP8X4),
                    lhsT_scale=term_scales[:, b * P : (b + 1) * P],
                    rhs=wd_q[h][0][:].bitcast(FP8X4),
                    rhs_scale=wd_q[h][1][:],
                    start=True,
                    stop=True,
                )
            root = sb(f"root{h}", [P, R_BLOCKS, VH], F32)
            numer = sb(f"numer{h}", [P, R_BLOCKS, VH], F32)
            inverse = sb(f"inverse{h}", [P, R_BLOCKS, VH], F32)
            result = sb(f"result{h}", [P, R_BLOCKS, VH], F32)
            nc.scalar.activation(out=root[:], in_=fb[:], func=ACT.Abs_reciprocal_sqrt, bias=SATURATION)
            for b in range(R_BLOCKS):
                nc.vector.scalar_tensor_tensor(
                    out=numer[:, b, :], in0=fb[:, b, :], scalar=idf_sb[:, b : b + 1],
                    in1=orig_sb[:, b, cols], op0=ALU.mult, op1=ALU.mult,
                )
            nc.scalar.activation(out=inverse[:], in_=root[:], func=ACT.Square)
            nc.vector.tensor_tensor(out=result[:], in0=numer[:], in1=inverse[:], op=ALU.mult)
            nc.sync.dma_start(out=out_rows[:, :, cols], in_=result[:])
